import numpy as np, ml_dtypes
CORES = [6,14,22,30,38,134,142,150,158]
N = 9
TK = 128
def silu(z): return z / (1.0 + np.exp(-z))
def setup_inputs(rng):
    return {"x": rng.standard_normal((N, 128, TK), dtype=np.float32).astype(ml_dtypes.bfloat16), "w1": (rng.standard_normal((N, 128, 128), dtype=np.float32) / 8).astype(ml_dtypes.bfloat16), "w3": (rng.standard_normal((N, 128, 128), dtype=np.float32) / 8).astype(ml_dtypes.bfloat16), "w2": (rng.standard_normal((N, 128, 128), dtype=np.float32) / 8).astype(ml_dtypes.bfloat16)}
def setup_inputs_big(rng):
    d = setup_inputs(rng)
    for k in ("x",): d[k] = (d[k].astype(np.float32) * 1024.0).astype(d[k].dtype)
    return d
def setup_inputs_small(rng):
    d = setup_inputs(rng)
    for k in ("x",): d[k] = (d[k].astype(np.float32) * (1 / 1024.0)).astype(d[k].dtype)
    return d
def setup_inputs_apart(rng):
    d = setup_inputs(rng)
    f = (10.0 ** rng.permutation(np.linspace(-1.5, 1.5, N))).astype(np.float32).reshape(N, 1, 1)
    for k in ("x",): d[k] = (d[k].astype(np.float32) * f).astype(d[k].dtype)
    return d
def reference(x, w1, w3, w2):
    X, W1, W3, W2 = x.astype(np.float64), w1.astype(np.float64), w3.astype(np.float64), w2.astype(np.float64)
    y = np.zeros((N, 128, TK))
    for r in range(N):
        for j in range(N):
            y[r] += W2[j].T @ (silu(W1[j].T @ X[r]) * (W3[j].T @ X[r]))
    return {"y": y.astype(ml_dtypes.bfloat16)}

@@ -1,0 +1,83 @@
+from concourse.mybir import AluOpType, ActivationFunctionType
+
+N = 9
+D = 128
+W = 3 * D
+NB = 3
+
+SCRATCH = {
+    "wall": ("sbuf", [128, N * W], "bfloat16"),
+    "xs": ("sbuf", [128, D], "bfloat16"),
+    "sil": ("sbuf", [128, N * D], "float32"),
+    "hs": ("sbuf", [128, N * D], "bfloat16"),
+    "ys": ("sbuf", [128, D], "bfloat16"),
+    "py": ("psum", [128, 512], "float32"),
+}
+for _b in range(NB):
+    SCRATCH["pa%d" % _b] = ("psum", [128, 512], "float32")
+    SCRATCH["pb%d" % _b] = ("psum", [128, 512], "float32")
+
+SEMAPHORES = ["wl", "xl", "sent", "yd", "yc", "st"]
+SEMAPHORES += ["a%d" % j for j in range(N)]
+SEMAPHORES += ["%s%d" % (c, k) for c in "pqsh" for k in range(N)]
+
+
+def rank_program(g, core, T, topo):
+    r = T.rank_of(core)
+    if r is None:
+        return
+    S = T.sem
+    o = r * W
+
+    g.sync.dma_start(T.wall[:, o:o + D], T.w1[:]).then_inc(S.wl, 16)
+    g.scalar.dma_start(T.wall[:, o + D:o + 2 * D], T.w3[:]).then_inc(S.wl, 16)
+    g.sync.dma_start(T.wall[:, o + 2 * D:o + W], T.w2[:]).then_inc(S.wl, 16)
+    g.scalar.dma_start(T.xs[:], T.x[:]).then_inc(S.xl, 16)
+
+    g.wait_ge(S.wl, 48)
+    left = 0
+    for s in range(1, N):
+        d = T.cores[(r + s) % N]
+        rid, pid = topo.addr(d, core)
+        m = topo.mask(core, d)
+        g.remote_dma(T.wall[:, o:o + W], T.wall[:, o:o + W], S["a%d" % r], S.sent, pid, rid, m)
+        left += bin(m).count("1")
+
+    order = [r] + [(r - s) % N for s in range(1, N)]
+    te, ac, ve = g.tensor, g.scalar, g.vector
+
+    def fold(k):
+        j = order[k]
+        te.wait_ge(S["h%d" % k], 1)
+        mm = te.matmul(T.py[:, 0:D], T.wall[:, j * W + 2 * D:j * W + W], T.hs[:, k * D:(k + 1) * D], k == 0, k == N - 1)
+        if k == N - 1:
+            mm.then_inc(S.yd, 1)
+
+    te.wait_ge(S.xl, 16)
+    for k, j in enumerate(order):
+        pa, pb = T["pa%d" % (k % NB)], T["pb%d" % (k % NB)]
+        if k == 0:
+            te.wait_ge(S.wl, 48)
+        else:
+            src = T.cores[j]
+            te.wait_ge(S["a%d" % j], bin(topo.mask(src, core)).count("1"))
+        te.matmul(pa[:, 0:D], T.wall[:, j * W:j * W + D], T.xs[:], True, True).then_inc(S["p%d" % k], 1)
+        te.matmul(pb[:, 0:D], T.wall[:, j * W + D:j * W + 2 * D], T.xs[:], True, True).then_inc(S["q%d" % k], 1)
+        if k >= 1:
+            fold(k - 1)
+
+        ac.wait_ge(S["p%d" % k], 1)
+        ac.activation(T.sil[:, k * D:(k + 1) * D], pa[:, 0:D], ActivationFunctionType.Silu).then_inc(S["s%d" % k], 1)
+
+        ve.wait_ge(S["s%d" % k], 1)
+        ve.wait_ge(S["q%d" % k], 1)
+        ve.tensor_tensor(T.hs[:, k * D:(k + 1) * D], T.sil[:, k * D:(k + 1) * D], pb[:, 0:D],
+                         AluOpType.mult).then_inc(S["h%d" % k], 1)
+    fold(N - 1)
+
+    ve.wait_ge(S.yd, 1)
+    ve.tensor_copy(T.ys[:], T.py[:, 0:D]).then_inc(S.yc, 1)
+    g.sync.wait_ge(S.yc, 1)
+    g.sync.dma_start(T.y[:], T.ys[:]).then_inc(S.st, 16)
+    g.sync.wait_ge(S.st, 16)
+    g.wait_ge(S.sent, left)

@@ -1,9 +1,12 @@
 from concourse.mybir import AluOpType, ActivationFunctionType
 
 N = 9
+NCORES = 256
 D = 128
 W = 3 * D
 NB = 3
+
+SHARE = [[1, 3, 5, 7], [2, 4, 6, 8]]
 
 SCRATCH = {
     "wall": ("sbuf", [128, N * W], "bfloat16"),
@@ -17,54 +20,118 @@ for _b in range(NB):
     SCRATCH["pa%d" % _b] = ("psum", [128, 512], "float32")
     SCRATCH["pb%d" % _b] = ("psum", [128, 512], "float32")
 
-SEMAPHORES = ["wl", "xl", "sent", "yd", "yc", "st"]
+SEMAPHORES = ["l2", "lp", "xl", "sent", "yd", "yc", "st"]
 SEMAPHORES += ["a%d" % j for j in range(N)]
+SEMAPHORES += ["b%d" % j for j in range(N)]
 SEMAPHORES += ["%s%d" % (c, k) for c in "pqsh" for k in range(N)]
 
 
+def _bits(m):
+    return bin(m).count("1")
+
+
+def _same_chip(topo, a, b):
+    return topo.host(a) == topo.host(b) and topo.chip(a) == topo.chip(b)
+
+
+def _helpers(T, topo, rc):
+    r = T.rank_of(rc)
+    free = [c for c in range(NCORES)
+            if _same_chip(topo, c, rc) and T.rank_of(c) is None and topo.die(c) != topo.die(rc)]
+    out = []
+    for share in SHARE:
+        ok = [c for c in free if c not in out and all(topo.may_write(c, T.cores[(r + s) % N]) for s in share)]
+        out.append(ok[0])
+    return out
+
+
+def _carrier(T, topo, j, s):
+    return [h for h, share in zip(_helpers(T, topo, T.cores[j]), SHARE) if s in share][0]
+
+
+def _chip_mask(T, topo, rc, h):
+    m = topo.mask(rc, h)
+    for d in T.cores:
+        if d != rc:
+            m &= topo.mask(rc, d)
+    return m
+
+
+def _send(g, T, topo, core, ap, sem, d):
+    rid, pid = topo.addr(d, core)
+    m = topo.mask(core, d)
+    g.remote_dma(ap, ap, sem, T.sem.sent, pid, rid, m)
+    return _bits(m)
+
+
 def rank_program(g, core, T, topo):
+    S = T.sem
+
+    def first(j):
+        return T.wall[:, j * W:j * W + 2 * D]
+
+    def last(j):
+        return T.wall[:, j * W + 2 * D:j * W + W]
+
     r = T.rank_of(core)
     if r is None:
+        for rc in T.cores:
+            if _same_chip(topo, rc, core):
+                hs = _helpers(T, topo, rc)
+                if core in hs:
+                    j = T.rank_of(rc)
+                    g.wait_ge(S["b%d" % j], _bits(_chip_mask(T, topo, rc, core)))
+                    left = 0
+                    for s in SHARE[hs.index(core)]:
+                        left += _send(g, T, topo, core, last(j), S["b%d" % j], T.cores[(j + s) % N])
+                    g.wait_ge(S.sent, left)
         return
-    S = T.sem
+
     o = r * W
 
-    g.sync.dma_start(T.wall[:, o:o + D], T.w1[:]).then_inc(S.wl, 16)
-    g.scalar.dma_start(T.wall[:, o + D:o + 2 * D], T.w3[:]).then_inc(S.wl, 16)
-    g.sync.dma_start(T.wall[:, o + 2 * D:o + W], T.w2[:]).then_inc(S.wl, 16)
-    g.scalar.dma_start(T.xs[:], T.x[:]).then_inc(S.xl, 16)
+    g.sync.dma_start(last(r), T.w2[:]).then_inc(S.l2, 16)
+    g.scalar.dma_start(T.wall[:, o:o + D], T.w1[:]).then_inc(S.lp, 16)
+    g.sync.dma_start(T.wall[:, o + D:o + 2 * D], T.w3[:]).then_inc(S.lp, 16)
+    g.sync.dma_start(T.xs[:], T.x[:]).then_inc(S.xl, 16)
 
-    g.wait_ge(S.wl, 48)
     left = 0
+    g.wait_ge(S.l2, 16)
+    for h in _helpers(T, topo, core):
+        rid, pid = topo.addr(h, core)
+        m = _chip_mask(T, topo, core, h)
+        g.remote_dma(last(r), last(r), S["b%d" % r], S.sent, pid, rid, m)
+        left += _bits(m)
+    g.wait_ge(S.lp, 32)
     for s in range(1, N):
-        d = T.cores[(r + s) % N]
-        rid, pid = topo.addr(d, core)
-        m = topo.mask(core, d)
-        g.remote_dma(T.wall[:, o:o + W], T.wall[:, o:o + W], S["a%d" % r], S.sent, pid, rid, m)
-        left += bin(m).count("1")
+        left += _send(g, T, topo, core, first(r), S["a%d" % r], T.cores[(r + s) % N])
 
-    order = [r] + [(r - s) % N for s in range(1, N)]
     te, ac, ve = g.tensor, g.scalar, g.vector
 
     def fold(k):
-        j = order[k]
+        j = (r - k) % N
+        if k == 0:
+            te.wait_ge(S.l2, 16)
+        else:
+            te.wait_ge(S["b%d" % j], _bits(topo.mask(_carrier(T, topo, j, k), core)))
         te.wait_ge(S["h%d" % k], 1)
-        mm = te.matmul(T.py[:, 0:D], T.wall[:, j * W + 2 * D:j * W + W], T.hs[:, k * D:(k + 1) * D], k == 0, k == N - 1)
+        mm = te.matmul(T.py[:, 0:D], last(j), T.hs[:, k * D:(k + 1) * D], k == 0, k == N - 1)
         if k == N - 1:
             mm.then_inc(S.yd, 1)
 
     te.wait_ge(S.xl, 16)
-    for k, j in enumerate(order):
+    for k in range(N):
+        j = (r - k) % N
         pa, pb = T["pa%d" % (k % NB)], T["pb%d" % (k % NB)]
         if k == 0:
-            te.wait_ge(S.wl, 48)
+            te.wait_ge(S.lp, 32)
         else:
-            src = T.cores[j]
-            te.wait_ge(S["a%d" % j], bin(topo.mask(src, core)).count("1"))
+            te.wait_ge(S["a%d" % j], _bits(topo.mask(T.cores[j], core)))
+        if k >= NB:
+            te.wait_ge(S["h%d" % (k - NB)], 1)
         te.matmul(pa[:, 0:D], T.wall[:, j * W:j * W + D], T.xs[:], True, True).then_inc(S["p%d" % k], 1)
         te.matmul(pb[:, 0:D], T.wall[:, j * W + D:j * W + 2 * D], T.xs[:], True, True).then_inc(S["q%d" % k], 1)
-        if k >= 1:
-            fold(k - 1)
+        if k == 1:
+            fold(0)
 
         ac.wait_ge(S["p%d" % k], 1)
         ac.activation(T.sil[:, k * D:(k + 1) * D], pa[:, 0:D], ActivationFunctionType.Silu).then_inc(S["s%d" % k], 1)
@@ -73,7 +140,8 @@ def rank_program(g, core, T, topo):
         ve.wait_ge(S["q%d" % k], 1)
         ve.tensor_tensor(T.hs[:, k * D:(k + 1) * D], T.sil[:, k * D:(k + 1) * D], pb[:, 0:D],
                          AluOpType.mult).then_inc(S["h%d" % k], 1)
-    fold(N - 1)
+    for k in range(1, N):
+        fold(k)
 
     ve.wait_ge(S.yd, 1)
     ve.tensor_copy(T.ys[:], T.py[:, 0:D]).then_inc(S.yc, 1)

from concourse.mybir import AluOpType, ActivationFunctionType

N = 9
NCORES = 256
D = 128
W = 3 * D
NB = 3

SHARE = [[1, 3, 5, 7], [2, 4, 6, 8]]

SCRATCH = {
    "wall": ("sbuf", [128, N * W], "bfloat16"),
    "xs": ("sbuf", [128, D], "bfloat16"),
    "sil": ("sbuf", [128, N * D], "float32"),
    "hs": ("sbuf", [128, N * D], "bfloat16"),
    "ys": ("sbuf", [128, D], "bfloat16"),
    "py": ("psum", [128, 512], "float32"),
}
for _b in range(NB):
    SCRATCH["pa%d" % _b] = ("psum", [128, 512], "float32")
    SCRATCH["pb%d" % _b] = ("psum", [128, 512], "float32")

SEMAPHORES = ["l2", "lp", "xl", "sent", "yd", "yc", "st"]
SEMAPHORES += ["a%d" % j for j in range(N)]
SEMAPHORES += ["b%d" % j for j in range(N)]
SEMAPHORES += ["%s%d" % (c, k) for c in "pqsh" for k in range(N)]


def _bits(m):
    return bin(m).count("1")


def _same_chip(topo, a, b):
    return topo.host(a) == topo.host(b) and topo.chip(a) == topo.chip(b)


def _helpers(T, topo, rc):
    r = T.rank_of(rc)
    free = [c for c in range(NCORES)
            if _same_chip(topo, c, rc) and T.rank_of(c) is None and topo.die(c) != topo.die(rc)]
    out = []
    for share in SHARE:
        ok = [c for c in free if c not in out and all(topo.may_write(c, T.cores[(r + s) % N]) for s in share)]
        out.append(ok[0])
    return out


def _carrier(T, topo, j, s):
    return [h for h, share in zip(_helpers(T, topo, T.cores[j]), SHARE) if s in share][0]


def _chip_mask(T, topo, rc, h):
    m = topo.mask(rc, h)
    for d in T.cores:
        if d != rc:
            m &= topo.mask(rc, d)
    return m


def _send(g, T, topo, core, ap, sem, d):
    rid, pid = topo.addr(d, core)
    m = topo.mask(core, d)
    g.remote_dma(ap, ap, sem, T.sem.sent, pid, rid, m)
    return _bits(m)


def rank_program(g, core, T, topo):
    S = T.sem

    def first(j):
        return T.wall[:, j * W:j * W + 2 * D]

    def last(j):
        return T.wall[:, j * W + 2 * D:j * W + W]

    r = T.rank_of(core)
    if r is None:
        for rc in T.cores:
            if _same_chip(topo, rc, core):
                hs = _helpers(T, topo, rc)
                if core in hs:
                    j = T.rank_of(rc)
                    g.wait_ge(S["b%d" % j], _bits(_chip_mask(T, topo, rc, core)))
                    left = 0
                    for s in SHARE[hs.index(core)]:
                        left += _send(g, T, topo, core, last(j), S["b%d" % j], T.cores[(j + s) % N])
                    g.wait_ge(S.sent, left)
        return

    o = r * W

    g.sync.dma_start(last(r), T.w2[:]).then_inc(S.l2, 16)
    g.scalar.dma_start(T.wall[:, o:o + D], T.w1[:]).then_inc(S.lp, 16)
    g.sync.dma_start(T.wall[:, o + D:o + 2 * D], T.w3[:]).then_inc(S.lp, 16)
    g.sync.dma_start(T.xs[:], T.x[:]).then_inc(S.xl, 16)

    left = 0
    g.wait_ge(S.l2, 16)
    for h in _helpers(T, topo, core):
        rid, pid = topo.addr(h, core)
        m = _chip_mask(T, topo, core, h)
        g.remote_dma(last(r), last(r), S["b%d" % r], S.sent, pid, rid, m)
        left += _bits(m)
    g.wait_ge(S.lp, 32)
    for s in range(1, N):
        left += _send(g, T, topo, core, first(r), S["a%d" % r], T.cores[(r + s) % N])

    te, ac, ve = g.tensor, g.scalar, g.vector

    def fold(k):
        j = (r - k) % N
        if k == 0:
            te.wait_ge(S.l2, 16)
        else:
            te.wait_ge(S["b%d" % j], _bits(topo.mask(_carrier(T, topo, j, k), core)))
        te.wait_ge(S["h%d" % k], 1)
        mm = te.matmul(T.py[:, 0:D], last(j), T.hs[:, k * D:(k + 1) * D], k == 0, k == N - 1)
        if k == N - 1:
            mm.then_inc(S.yd, 1)

    te.wait_ge(S.xl, 16)
    for k in range(N):
        j = (r - k) % N
        pa, pb = T["pa%d" % (k % NB)], T["pb%d" % (k % NB)]
        if k == 0:
            te.wait_ge(S.lp, 32)
        else:
            te.wait_ge(S["a%d" % j], _bits(topo.mask(T.cores[j], core)))
        if k >= NB:
            te.wait_ge(S["h%d" % (k - NB)], 1)
        te.matmul(pa[:, 0:D], T.wall[:, j * W:j * W + D], T.xs[:], True, True).then_inc(S["p%d" % k], 1)
        te.matmul(pb[:, 0:D], T.wall[:, j * W + D:j * W + 2 * D], T.xs[:], True, True).then_inc(S["q%d" % k], 1)
        if k == 1:
            fold(0)

        ac.wait_ge(S["p%d" % k], 1)
        ac.activation(T.sil[:, k * D:(k + 1) * D], pa[:, 0:D], ActivationFunctionType.Silu).then_inc(S["s%d" % k], 1)

        ve.wait_ge(S["s%d" % k], 1)
        ve.wait_ge(S["q%d" % k], 1)
        ve.tensor_tensor(T.hs[:, k * D:(k + 1) * D], T.sil[:, k * D:(k + 1) * D], pb[:, 0:D],
                         AluOpType.mult).then_inc(S["h%d" % k], 1)
    for k in range(1, N):
        fold(k)

    ve.wait_ge(S.yd, 1)
    ve.tensor_copy(T.ys[:], T.py[:, 0:D]).then_inc(S.yc, 1)
    g.sync.wait_ge(S.yc, 1)
    g.sync.dma_start(T.y[:], T.ys[:]).then_inc(S.st, 16)
    g.sync.wait_ge(S.st, 16)
    g.wait_ge(S.sent, left)
